import numpy as np
import ml_dtypes


def mxq(x, axis, fmt="e4m3"):
    dtype, down = {"e4m3": (ml_dtypes.float8_e4m3fn, 7), "e5m2": (ml_dtypes.float8_e5m2, 14)}[fmt]
    v = np.moveaxis(np.asarray(x, np.float32).astype(ml_dtypes.bfloat16).astype(np.float64), axis, -1)
    blocks = v.reshape(v.shape[:-1] + (-1, 32))
    amax = np.abs(blocks).max(-1, keepdims=True)
    byte = np.maximum(np.where(amax > 0, np.frexp(amax)[1] - 1 + 127, 0) - down, 1)
    scale = np.exp2(byte - 127.0)
    codes = (blocks / scale).astype(np.float32).astype(dtype).astype(np.float64)
    return np.moveaxis((codes * scale).reshape(v.shape), -1, axis)


WIDE = False


def mx_kscale(k):
    if not WIDE:
        return np.ones(k)
    levels = np.array([10, -10, 5, -5, 0])
    if k % 512:
        return np.exp2(np.random.permutation(np.resize(levels, k // 32))).repeat(32)
    a = np.empty((k // 512, 16))
    for p in range(k // 512):
        a[p, :8] = np.random.permutation(np.resize(levels, 8))
        for g in range(8):
            far = levels[np.abs(levels - a[p, g]) >= 10]
            a[p, g + 8] = far[np.random.randint(len(far))]
    return np.exp2(a.ravel()).repeat(32)


def f64(x):
    return np.asarray(x).astype(np.float64)


def striped(idx):
    return np.tile(idx.reshape(-1, 16).T, (8, 1)).astype(np.uint16)


def unstriped(offs):
    return offs[:16].T.reshape(-1).astype(np.int64)


def striped8(idx):
    return np.concatenate([x.reshape(-1, 16).T for x in idx]).astype(np.uint16)


def runs(offs, k):
    lists = np.stack([offs[16 * r : 16 * r + 16].T.reshape(-1) for r in range(8)]).astype(np.int64)
    return lists[np.arange(k) % 512 // 64]


def pack_weight(w):
    k, n = w.shape
    w = f64(np.asarray(w, np.float32).astype(ml_dtypes.bfloat16)).reshape(k // 32, 32, n)
    amax = np.abs(w).max(1)
    byte = np.clip(np.where(amax > 0, np.frexp(amax)[1] - 1 + 127 - 7, 1), 1, 254)
    scaled = (w * np.exp2(127.0 - byte)[:, None, :]).reshape(k, n).astype(np.float32)
    words = np.ascontiguousarray(scaled.reshape(k // 512, 128, 4, n).transpose(0, 1, 3, 2)).astype(ml_dtypes.float8_e4m3fn).view(np.uint8)
    return words, np.ascontiguousarray(byte.astype(np.uint8).reshape(k // 512, 16, n))


def unpack_weight(words, scales):
    g, p, n, _ = words.shape
    vals = np.ascontiguousarray(words).view(ml_dtypes.float8_e4m3fn).astype(np.float64) * np.repeat(np.exp2(scales.astype(np.float64) - 127.0), 8, axis=1)[..., None]
    return vals.transpose(0, 1, 3, 2).reshape(g * 512, n)


def sigmoid(v):
    return 1.0 / (1.0 + np.exp(-np.maximum(v, -700.0)))

def planes(y):
    n, m = y.shape
    v = y.astype(np.float32).astype(ml_dtypes.bfloat16).astype(np.float64).reshape(n // 32, 32, m)
    top = np.abs(v).max(1)
    byte = np.clip(np.where(top > 0, np.frexp(top)[1] - 1 + 127 - 7, 1), 1, 254)
    codes = (v * np.exp2(127.0 - byte)[:, None, :]).reshape(n, m).astype(np.float32).astype(ml_dtypes.float8_e4m3fn).view(np.uint8)
    words = codes.reshape(n // 512, 128, 4, m).transpose(0, 1, 3, 2)
    return np.ascontiguousarray(words), np.ascontiguousarray(byte.astype(np.uint8).reshape(n // 512, 16, m))


K, T, S, G, H, W, C = 512, 1024, 256, 2048, 512, 128, 512


def setup_inputs():
    n = np.random.standard_normal
    s = mx_kscale(K)[:, None]
    packed_xT = pack_weight(n((K, T)) * s)
    packed_dT = pack_weight(n((K, G)) / s)
    perm = np.random.permutation(S)
    perm2 = np.random.permutation(S)
    perm3 = np.random.permutation(S)
    perm4 = np.random.permutation(S)
    return {
        "x_words": packed_xT[0],
        "x_scales": packed_xT[1],
        "d_words": packed_dT[0],
        "d_scales": packed_dT[1],
        "sl": np.random.uniform(1.0, 2.0, (H, 1)).astype(np.float32),
        "th": (0.5 * n((H, 1))).astype(np.float32),
        "gs": (np.random.uniform(0.5, 1.5, (K, 1)) / s).astype(np.float32),
        "offs": striped(np.random.permutation(T)[:S]),
        "k1": striped8(np.random.randint(0, G, (8, H))),
        "two": striped(np.random.permutation(T)[:S]),
        "k2": striped8(np.random.randint(0, G, (8, H))),
        "hz": striped8(np.random.randint(0, T, (8, S))),
        "k3": striped8(np.random.randint(0, G, (8, H))),
        "n1": striped(perm[:W]),
        "n2": striped(perm[W:]),
        "n3": striped(perm2[:W]),
        "n4": striped(perm2[W:]),
        "n5": striped(np.random.permutation(S)),
        "cand": striped(np.random.permutation(T)[:C]),
        "n6": striped(perm3[:W]),
        "n7": striped(perm3[W:]),
        "n8": striped(perm4[:W]),
        "n9": striped(perm4[W:]),
        "n10": striped(np.random.permutation(S)),
    }


def reference(x_words, x_scales, d_words, d_scales, sl, th, gs, offs, k1, two, k2, hz, k3, n1, n2, n3, n4, n5, cand, n6, n7, n8, n9, n10):
    x_cand = unpack_weight(x_words, x_scales)[:, unstriped(cand)]
    d_k1 = unpack_weight(d_words, d_scales)[np.arange(K)[:, None], runs(k1, K)]
    xq = unpack_weight(x_words, x_scales)[:, unstriped(offs)]
    d_k2 = unpack_weight(d_words, d_scales)[np.arange(K)[:, None], runs(k2, K)]
    x_two = unpack_weight(x_words, x_scales)[:, unstriped(two)]
    d_k3 = unpack_weight(d_words, d_scales)[np.arange(K)[:, None], runs(k3, K)]
    x_hz = unpack_weight(x_words, x_scales)[np.arange(K)[:, None], runs(hz, K)]
    h = 0.0625 * (d_k1.T @ xq + d_k2.T @ x_two + d_k3.T @ x_hz)
    pa = h[:, unstriped(n1)]
    pb = h[:, unstriped(n2)]
    rb = np.minimum(pa, pb)
    ra = np.maximum(pa, pb)
    ua = np.zeros((H, S))
    ua[:, unstriped(n3)] = ra
    ub = ua.copy()
    ub[:, unstriped(n4)] = rb
    sg = sigmoid(f64(sl) * (ub[:, unstriped(n5)] - f64(th)))
    z = f64(gs) * (ub * sg)
    s = 0.0625 * ((x_cand.T @ mxq(z, 0, "e4m3")))
    pa2 = s[:, unstriped(n6)]
    pb2 = s[:, unstriped(n7)]
    rb2 = np.maximum(pa2, pb2)
    ua2 = np.zeros((C, S))
    ua2[:, unstriped(n8)] = pb2
    ub2 = ua2.copy()
    ub2[:, unstriped(n9)] = rb2
    out_0 = ub2 - s[:, unstriped(n10)]
    return (out_0,) + planes(out_0)

@@ -1,0 +1,277 @@
+from contextlib import ExitStack
+
+import concourse.mybir as mybir
+from concourse.masks import make_identity
+
+K, T, S, G, H, W, C = 512, 1024, 256, 2048, 512, 128, 512
+FLOPS = 2 * K * S * (3 * H + C)
+
+F32 = mybir.dt.float32
+BF16 = mybir.dt.bfloat16
+I32 = mybir.dt.int32
+U32 = mybir.dt.uint32
+U16 = mybir.dt.uint16
+U8 = mybir.dt.uint8
+FP8X4 = mybir.dt.float8_e4m3fn_x4
+ALU = mybir.AluOpType
+ACT = mybir.ActivationFunctionType
+
+P = 128
+HALF = 256
+SIXTEENTH = 0.0625
+
+
+def tile_picked_mtthzceordcpsw_none_po_kernel(
+    tc, x_words, x_scales, d_words, d_scales, sl, th, gs, offs, k1, two, k2, hz, k3,
+    n1, n2, n3, n4, n5, cand, n6, n7, n8, n9, n10, out_0, out_1, out_2,
+):
+    nc = tc.nc
+    with ExitStack() as ctx:
+        lists = ctx.enter_context(tc.tile_pool(name="lists", bufs=1))
+        sb = ctx.enter_context(tc.tile_pool(name="sb", bufs=1))
+        psum = ctx.enter_context(tc.psum_pool(name="psum", bufs=1))
+
+        def tile(name, shape, dtype, tag=None):
+            return sb.tile(shape, dtype, name=name, tag=tag or name, align_bytes=64)
+
+        def load_list(name, source):
+            held = lists.tile(list(source.shape), U16, name=name, tag=name)
+            nc.sync.dma_start(held[:], source)
+            return held
+
+        d_bytes = tile("d_bytes", [P, G], U8)
+        x_bytes = tile("x_bytes", [P, T], U8)
+        nc.vector.memset(d_bytes[:].bitcast(I32), 0)
+        nc.vector.memset(x_bytes[:].bitcast(I32), 0)
+        nc.scalar.dma_start(d_bytes[:].bitcast(I32)[0:P:8, :], d_scales[0].bitcast(I32))
+        nc.scalar.dma_start(x_bytes[:].bitcast(I32)[0:P:8, :], x_scales[0].bitcast(I32))
+        L = {}
+        for name, source in (("k1", k1), ("k2", k2), ("k3", k3), ("hz", hz), ("offs", offs), ("two", two)):
+            L[name] = load_list(name, source)
+        x_tab = tile("x_tab", [P, T], U32)
+        d_tab = tile("d_tab", [P, G], U32)
+        nc.sync.dma_start(x_tab[:].bitcast(I32), x_words[0].rearrange("p n t -> p (n t)").bitcast(I32))
+        nc.sync.dma_start(d_tab[:].bitcast(I32), d_words[0].rearrange("p n t -> p (n t)").bitcast(I32))
+        for name, source in (("n1", n1), ("n2", n2), ("n3", n3), ("n4", n4), ("n5", n5), ("cand", cand)):
+            L[name] = load_list(name, source)
+
+        slope = tile("slope", [P, 4], F32)
+        thresh = tile("thresh", [P, 4], F32)
+        gain = tile("gain", [P, 4], F32)
+        with nc.allow_non_contiguous_dma(reason="one float32 value a row"):
+            for held, source in ((slope, sl), (thresh, th), (gain, gs)):
+                nc.gpsimd.dma_start(held[:], source.rearrange("(u p) o -> p (u o)", p=P))
+        slope_thresh = tile("slope_thresh", [P, 4], F32)
+        bias = tile("bias", [P, 4], F32)
+        nc.gpsimd.tensor_tensor(slope_thresh[:], slope[:], thresh[:], ALU.mult)
+        nc.gpsimd.tensor_scalar(bias[:], slope_thresh[:], -1.0, 0.0, ALU.mult, ALU.add)
+        ident = tile("ident", [P, P], F32)
+        make_identity(nc, ident[:])
+
+        planes_a = tile("planes_a", [P, 6 * HALF], U8)
+        planes_b = tile("planes_b", [P, 3 * HALF], U8)
+        planes_c = tile("planes_c", [P, C], U8)
+        for plane in (planes_a, planes_b, planes_c):
+            nc.vector.memset(plane[:].bitcast(I32), 0)
+
+        def seat_rows(queue, plane, picked):
+            for s in range(4):
+                queue.dma_start(plane[:].bitcast(I32)[s:P:32, :], picked[:].bitcast(I32)[8 * s:P:32, :])
+
+        def part(name, half):
+            return L[name][:, 16 * half:16 * (half + 1)]
+
+        d_names = ("k1", "k2", "k3")
+        x_names = ("offs", "two", "hz")
+
+        picked_a = tile("picked_a", [P, 6 * HALF], U8, tag="picked")
+        for g, name in enumerate(d_names):
+            nc.vector.tensor_copy(picked_a[:, g * HALF:(g + 1) * HALF], d_bytes[:].indirect(part(name, 0)))
+        for g in (2, 0, 1):
+            nc.vector.tensor_copy(picked_a[:, (3 + g) * HALF:(4 + g) * HALF], x_bytes[:].indirect(L[x_names[g]][:]))
+        seat_rows(nc.scalar, planes_a, picked_a)
+        x_pick = []
+        for name in x_names:
+            words = tile("xw_" + name, [P, S], U32)
+            nc.vector.tensor_copy(words[:], x_tab[:].indirect(L[name][:]))
+            x_pick.append(words)
+
+        def first_product(d_pick, planes, acc):
+            for v in range(2):
+                for g in range(3):
+                    cols = slice(g * HALF + v * P, g * HALF + (v + 1) * P)
+                    nc.tensor.matmul_mx(
+                        out=acc[v][:], lhsT=d_pick[g][:, v * P:(v + 1) * P].bitcast(FP8X4), lhsT_scale=planes[:, cols],
+                        rhs=x_pick[g][:].bitcast(FP8X4), rhs_scale=planes_a[:, (3 + g) * HALF:(4 + g) * HALF],
+                        start=(g == 0), stop=(g == 2))
+
+        def pick_words(half, tags):
+            picked = []
+            for name, tag in zip(d_names, tags):
+                words = tile(f"dw_{name}_{half}", [P, HALF], U32, tag=tag)
+                nc.vector.tensor_copy(words[:], d_tab[:].indirect(part(name, half)))
+                picked.append(words)
+            return picked
+
+        d_pick_a = pick_words(0, (None, None, None))
+        acc = [psum.tile([P, S], F32, name=f"h_acc{u}", tag=f"acc{u}") for u in range(2)]
+        first_product(d_pick_a, planes_a, acc)
+
+        picked_b = tile("picked_b", [P, 3 * HALF], U8, tag="picked")
+        for g, name in enumerate(d_names):
+            nc.vector.tensor_copy(picked_b[:, g * HALF:(g + 1) * HALF], d_bytes[:].indirect(part(name, 1)))
+        seat_rows(nc.sync, planes_b, picked_b)
+
+        turned = [psum.tile([P, 4, P], F32, name=f"turned{a}", tag=f"turned{a}") for a in range(2)]
+        z_rows = [tile(f"z_rows{a}", [P, 2, P, 2], BF16) for a in range(2)]
+
+        def fetch_pair(u, source):
+            h = tile(f"h{u}", [P, S], F32)
+            if u == 0:
+                nc.scalar.activation(h[:], source[:], ACT.Copy, scale=SIXTEENTH)
+            else:
+                nc.vector.tensor_scalar(h[:], source[:], SIXTEENTH, None, ALU.mult)
+            pair = tile(f"pair{u}", [P, 2, W], F32)
+            nc.scalar.activation(pair[:, 0, :], h[:].indirect(L["n1"][:]), ACT.Copy)
+            nc.scalar.activation(pair[:, 1, :], h[:].indirect(L["n2"][:]), ACT.Copy)
+            return pair
+
+        def rank(u, pairs):
+            high = [tile(f"high{u + v}", [P, W], F32) for v in range(2)]
+            low = [tile(f"low{u}", [P, W], F32, tag=f"h{u + 1}"), tile(f"low{u + 1}", [P, W], F32)]
+            for v in range(2):
+                nc.vector.tensor_tensor(high[v][:], pairs[v][:, 0, :], pairs[v][:, 1, :], ALU.max)
+            for v in range(2):
+                nc.vector.tensor_tensor(low[v][:], pairs[v][:, 0, :], pairs[v][:, 1, :], ALU.min)
+            return high, low
+
+        def put_back(u, high, low):
+            ub = [tile(f"ub{u + v}", [P, S], F32) for v in range(2)]
+            for v in range(2):
+                nc.scalar.activation(ub[v][:].indirect(L["n3"][:]), high[v][:], ACT.Copy)
+            for v in range(2):
+                nc.scalar.activation(ub[v][:].indirect(L["n4"][:]), low[v][:], ACT.Copy)
+            return ub
+
+        def gate(u, a, ub, sg, z):
+            cols = slice(a * P, (a + 1) * P)
+            nc.scalar.activation(sg[:, cols], ub[:].indirect(L["n5"][:, 8 * a:8 * (a + 1)]), ACT.Sigmoid,
+                                 bias=bias[:, u:u + 1], scale=slope[:, u:u + 1])
+            nc.vector.scalar_tensor_tensor(z[:, cols], ub[:, cols], gain[:, u:u + 1], sg[:, cols], ALU.mult, ALU.mult)
+            nc.tensor.transpose(turned[a][:, u, :], z[:, cols], ident[:])
+
+        def regroup(a, lo, hi):
+            source = turned[a][:].rearrange("j u (q e b) -> j e (u q) b", e=2, b=2)
+            nc.vector.tensor_copy(z_rows[a][:, :, lo:hi, :], source[:, :, lo:hi, :])
+
+        ranked_a = rank(0, [fetch_pair(u, acc[u]) for u in range(2)])
+
+        d_pick_b = pick_words(1, ("h0", "pair0", "pair1"))
+        acc_b = [psum.tile([P, S], F32, name=f"h_acc{u}", tag=f"acc{u}") for u in range(2, 4)]
+        first_product(d_pick_b, planes_b, acc_b)
+
+        ub0, ub1 = put_back(0, *ranked_a)
+
+        ranked_b = rank(2, [fetch_pair(2 + v, acc_b[v]) for v in range(2)])
+
+        picked_c = tile("picked_c", [P, 4, P], U8, tag="pair2")
+        nc.vector.tensor_copy(picked_c[:].rearrange("p t m -> p m t"), x_bytes[:].indirect(L["cand"][:]))
+        for s in range(4):
+            nc.sync.dma_start(planes_c[:].bitcast(I32)[s:P:32, :],
+                              picked_c[:].rearrange("p t m -> p (t m)").bitcast(I32)[8 * s:P:32, :])
+        for name, source in (("n6", n6), ("n7", n7), ("n8", n8), ("n9", n9), ("n10", n10)):
+            L[name] = load_list(name, source)
+
+        sg0 = tile("sg0", [P, S], F32)
+        z0 = tile("z0", [P, S], F32, tag="pair1")
+        sg1 = tile("sg1", [P, S], F32, tag="h2")
+        z1 = tile("z1", [P, S], F32)
+        for a in range(2):
+            gate(0, a, ub0, sg0, z0)
+        for a in range(2):
+            gate(1, a, ub1, sg1, z1)
+
+        c_pick = tile("c_pick", [P, 4, P], U32, tag="pair3")
+        for half in range(2):
+            nc.vector.tensor_copy(c_pick[:].rearrange("p t m -> p m t")[:, 64 * half:64 * (half + 1), :],
+                                  x_tab[:].indirect(part("cand", half)))
+
+        ub2, ub3 = put_back(2, *ranked_b)
+        late = [(u, ub, tile(f"sg{u}", [P, S], F32), tile(f"z{u}", [P, S], F32)) for u, ub in ((2, ub2), (3, ub3))]
+        for a in range(2):
+            for u, ub, sg, z in late:
+                gate(u, a, ub, sg, z)
+                if u == 2:
+                    regroup(a, 0, 96)
+                else:
+                    regroup(a, 96, 128)
+
+        z_codes = tile("z_codes", [P, S], U32)
+        z_scales = tile("z_scales", [P, S], U8)
+        s_acc = [psum.tile([P, S], F32, name=f"s_acc{t}", tag=f"acc{t}") for t in range(4)]
+        scores = [tile(f"scores{t}", [P, S], F32) for t in range(4)]
+        for a in range(2):
+            cols = slice(a * P, (a + 1) * P)
+            back = psum.tile([P, 2, P], F32, name=f"back{a}", tag=f"back{a}")
+            pairs = z_rows[a][:].rearrange("j e p b -> j (e p b)").bitcast(F32)
+            for e in range(2):
+                nc.tensor.transpose(back[:, e, :], pairs[:, e * P:(e + 1) * P], ident[:])
+            z_bf = tile(f"z_bf{a}", [P, 4 * P], BF16)
+            nc.vector.tensor_copy(z_bf[:].bitcast(F32).rearrange("p (j e) -> p j e", e=2),
+                                  back[:].rearrange("p e j -> p j e"))
+            nc.vector.quantize_mx(out=z_codes[:, cols].bitcast(FP8X4), scales=z_scales[:, cols], in_=z_bf[:])
+            for t in range(4):
+                nc.tensor.matmul_mx(
+                    out=s_acc[t][:, cols], lhsT=c_pick[:, t, :].bitcast(FP8X4),
+                    lhsT_scale=planes_c[:, t * P:(t + 1) * P],
+                    rhs=z_codes[:, cols].bitcast(FP8X4), rhs_scale=z_scales[:, cols], start=True, stop=True)
+            if a == 0:
+                nc.vector.tensor_scalar(scores[0][:, cols], s_acc[0][:, cols], SIXTEENTH, None, ALU.mult)
+            else:
+                nc.scalar.activation(scores[0][:, cols], s_acc[0][:, cols], ACT.Copy, scale=SIXTEENTH)
+        for t in range(1, 4):
+            nc.vector.tensor_scalar(scores[t][:], s_acc[t][:], SIXTEENTH, None, ALU.mult)
+
+        result = tile("result", [P, 4, S], F32)
+        rows = out_0.rearrange("(p t) j -> p t j", t=4)
+        def place(t):
+            pair = tile(f"s_pair{t}", [P, 2, W], F32)
+            nc.scalar.activation(pair[:, 0, :], scores[t][:].indirect(L["n6"][:]), ACT.Copy)
+            nc.scalar.activation(pair[:, 1, :], scores[t][:].indirect(L["n7"][:]), ACT.Copy)
+            larger = tile(f"larger{t}", [P, W], F32)
+            nc.vector.tensor_tensor(larger[:], pair[:, 0, :], pair[:, 1, :], ALU.max)
+            placed = tile(f"placed{t}", [P, S], F32)
+            nc.scalar.activation(placed[:].indirect(L["n8"][:]), pair[:, 1, :], ACT.Copy)
+            nc.scalar.activation(placed[:].indirect(L["n9"][:]), larger[:], ACT.Copy)
+            return placed
+
+        def subtract(t, placed):
+            other = tile(f"other{t}", [P, S], F32, tag="larger3" if t == 3 else None)
+            for a in range(2):
+                cols = slice(a * P, (a + 1) * P)
+                nc.scalar.activation(other[:, cols], scores[t][:].indirect(L["n10"][:, 8 * a:8 * (a + 1)]), ACT.Copy)
+                nc.vector.tensor_tensor(result[:, t, cols], placed[:, cols], other[:, cols], ALU.subtract)
+                if t == 3:
+                    nc.sync.dma_start(rows[:, t, cols], result[:, t, cols])
+            if t < 3:
+                nc.sync.dma_start(rows[:, t, :], result[:, t, :])
+
+        placed = [place(0)]
+        for t in range(1, 4):
+            placed.append(place(t))
+            subtract(t - 1, placed[t - 1])
+        subtract(3, placed[3])
+
+        y_codes = tile("y_codes", [P, S], U32)
+        y_scales = tile("y_scales", [P, S], U8)
+        codes_out = out_1[0].rearrange("p n t -> p (n t)").bitcast(I32)
+        for a in range(2):
+            cols = slice(a * P, (a + 1) * P)
+            y_bf = tile(f"y_bf{a}", [P, P, 4], BF16)
+            nc.vector.tensor_copy(y_bf[:], result[:, :, cols].rearrange("p t j -> p j t"))
+            nc.vector.quantize_mx(out=y_codes[:, cols].bitcast(FP8X4), scales=y_scales[:, cols],
+                                  in_=y_bf[:].rearrange("p j t -> p (j t)"))
+            nc.sync.dma_start(codes_out[:, cols], y_codes[:, cols].bitcast(I32))
+        for q in range(4):
+            queue = nc.sync if q % 2 else nc.scalar
+            queue.dma_start(out_2[0].bitcast(I32)[4 * q:4 * q + 4, :], y_scales[:].bitcast(I32)[32 * q:32 * q + 4, :])

@@ -45,6 +45,10 @@ def tile_picked_mtthzceordcpsw_none_po_kernel(
         nc.vector.memset(x_bytes[:].bitcast(I32), 0)
         nc.scalar.dma_start(d_bytes[:].bitcast(I32)[0:P:8, :], d_scales[0].bitcast(I32))
         nc.scalar.dma_start(x_bytes[:].bitcast(I32)[0:P:8, :], x_scales[0].bitcast(I32))
+        warm_in = tile("warm_in", [P, 1], F32)
+        warm_out = tile("warm_out", [P, 1], F32)
+        nc.vector.memset(warm_in[:], 0.0)
+        nc.scalar.activation(warm_out[:], warm_in[:], ACT.Sigmoid)
         L = {}
         for name, source in (("k1", k1), ("k2", k2), ("k3", k3), ("hz", hz), ("offs", offs), ("two", two)):
             L[name] = load_list(name, source)

@@ -41,24 +41,30 @@ def tile_picked_mtthzceordcpsw_none_po_kernel(
 
         d_bytes = tile("d_bytes", [P, G], U8)
         x_bytes = tile("x_bytes", [P, T], U8)
-        nc.vector.memset(d_bytes[:].bitcast(I32), 0)
+        nc.gpsimd.memset(d_bytes[:].bitcast(I32), 0)
         nc.vector.memset(x_bytes[:].bitcast(I32), 0)
-        nc.scalar.dma_start(d_bytes[:].bitcast(I32)[0:P:8, :], d_scales[0].bitcast(I32))
-        nc.scalar.dma_start(x_bytes[:].bitcast(I32)[0:P:8, :], x_scales[0].bitcast(I32))
+        nc.sync.dma_start(x_bytes[:].bitcast(I32)[0:P:8, :], x_scales[0].bitcast(I32))
         warm_in = tile("warm_in", [P, 1], F32)
         warm_out = tile("warm_out", [P, 1], F32)
         nc.vector.memset(warm_in[:], 0.0)
         nc.scalar.activation(warm_out[:], warm_in[:], ACT.Sigmoid)
         L = {}
-        for name, source in (("k1", k1), ("k2", k2), ("k3", k3), ("hz", hz), ("offs", offs), ("two", two)):
+        for name, source in (("hz", hz), ("offs", offs), ("two", two)):
+            L[name] = load_list(name, source)
+        nc.sync.dma_start(d_bytes[:].bitcast(I32)[0:P:8, :], d_scales[0].bitcast(I32))
+        for name, source in (("k1", k1), ("k2", k2), ("k3", k3)):
             L[name] = load_list(name, source)
         x_tab = tile("x_tab", [P, T], U32)
         d_tab = tile("d_tab", [P, G], U32)
         nc.sync.dma_start(x_tab[:].bitcast(I32), x_words[0].rearrange("p n t -> p (n t)").bitcast(I32))
-        nc.sync.dma_start(d_tab[:].bitcast(I32), d_words[0].rearrange("p n t -> p (n t)").bitcast(I32))
-        for name, source in (("n1", n1), ("n2", n2), ("n3", n3), ("n4", n4), ("n5", n5), ("cand", cand)):
-            L[name] = load_list(name, source)
+        d_source = d_words[0].rearrange("p n t -> p (n t)").bitcast(I32)
+        nc.gpsimd.dma_start(d_tab[:].bitcast(I32)[:, :G // 2], d_source[:, :G // 2])
+        nc.sync.dma_start(d_tab[:].bitcast(I32)[:, G // 2:], d_source[:, G // 2:])
 
+        wide_ub = [tile(f"ub{u}", [P, 2 * S], F32) for u in range(2)]
+        scores = [tile(f"scores{t}", [P, S + 32 if t < 3 else S], F32) for t in range(4)]
+        for window in wide_ub + scores[:3]:
+            nc.gpsimd.memset(window[:, S:], 0.0)
         slope = tile("slope", [P, 4], F32)
         thresh = tile("thresh", [P, 4], F32)
         gain = tile("gain", [P, 4], F32)
@@ -78,9 +84,9 @@ def tile_picked_mtthzceordcpsw_none_po_kernel(
         for plane in (planes_a, planes_b, planes_c):
             nc.vector.memset(plane[:].bitcast(I32), 0)
 
-        def seat_rows(queue, plane, picked):
+        def seat_rows(queues, plane, picked):
             for s in range(4):
-                queue.dma_start(plane[:].bitcast(I32)[s:P:32, :], picked[:].bitcast(I32)[8 * s:P:32, :])
+                queues[s % 2].dma_start(plane[:].bitcast(I32)[s:P:32, :], picked[:].bitcast(I32)[8 * s:P:32, :])
 
         def part(name, half):
             return L[name][:, 16 * half:16 * (half + 1)]
@@ -89,11 +95,13 @@ def tile_picked_mtthzceordcpsw_none_po_kernel(
         x_names = ("offs", "two", "hz")
 
         picked_a = tile("picked_a", [P, 6 * HALF], U8, tag="picked")
-        for g, name in enumerate(d_names):
-            nc.vector.tensor_copy(picked_a[:, g * HALF:(g + 1) * HALF], d_bytes[:].indirect(part(name, 0)))
         for g in (2, 0, 1):
             nc.vector.tensor_copy(picked_a[:, (3 + g) * HALF:(4 + g) * HALF], x_bytes[:].indirect(L[x_names[g]][:]))
-        seat_rows(nc.scalar, planes_a, picked_a)
+        for g, name in enumerate(d_names):
+            nc.vector.tensor_copy(picked_a[:, g * HALF:(g + 1) * HALF], d_bytes[:].indirect(part(name, 0)))
+        seat_rows((nc.scalar, nc.sync), planes_a, picked_a)
+        for name, source in (("n1", n1), ("n2", n2), ("n3", n3), ("n4", n4), ("n5", n5), ("cand", cand)):
+            L[name] = load_list(name, source)
         x_pick = []
         for name in x_names:
             words = tile("xw_" + name, [P, S], U32)
@@ -124,14 +132,13 @@ def tile_picked_mtthzceordcpsw_none_po_kernel(
         picked_b = tile("picked_b", [P, 3 * HALF], U8, tag="picked")
         for g, name in enumerate(d_names):
             nc.vector.tensor_copy(picked_b[:, g * HALF:(g + 1) * HALF], d_bytes[:].indirect(part(name, 1)))
-        seat_rows(nc.sync, planes_b, picked_b)
+        seat_rows((nc.sync, nc.sync), planes_b, picked_b)
 
-        turned = [psum.tile([P, 4, P], F32, name=f"turned{a}", tag=f"turned{a}") for a in range(2)]
-        z_rows = [tile(f"z_rows{a}", [P, 2, P, 2], BF16) for a in range(2)]
+        z_half = [None, None]
 
         def fetch_pair(u, source):
             h = tile(f"h{u}", [P, S], F32)
-            if u == 0:
+            if u < 2:
                 nc.scalar.activation(h[:], source[:], ACT.Copy, scale=SIXTEENTH)
             else:
                 nc.vector.tensor_scalar(h[:], source[:], SIXTEENTH, None, ALU.mult)
@@ -150,23 +157,22 @@ def tile_picked_mtthzceordcpsw_none_po_kernel(
             return high, low
 
         def put_back(u, high, low):
-            ub = [tile(f"ub{u + v}", [P, S], F32) for v in range(2)]
+            ub = wide_ub if u == 0 else [tile(f"ub{u + v}", [P, S], F32) for v in range(2)]
             for v in range(2):
                 nc.scalar.activation(ub[v][:].indirect(L["n3"][:]), high[v][:], ACT.Copy)
             for v in range(2):
                 nc.scalar.activation(ub[v][:].indirect(L["n4"][:]), low[v][:], ACT.Copy)
             return ub
 
-        def gate(u, a, ub, sg, z):
-            cols = slice(a * P, (a + 1) * P)
-            nc.scalar.activation(sg[:, cols], ub[:].indirect(L["n5"][:, 8 * a:8 * (a + 1)]), ACT.Sigmoid,
+        def squash(u, ub, sg, lo, hi):
+            nc.scalar.activation(sg[:, lo:hi], ub[:].indirect(L["n5"][:, lo // 16:hi // 16]), ACT.Sigmoid,
                                  bias=bias[:, u:u + 1], scale=slope[:, u:u + 1])
-            nc.vector.scalar_tensor_tensor(z[:, cols], ub[:, cols], gain[:, u:u + 1], sg[:, cols], ALU.mult, ALU.mult)
-            nc.tensor.transpose(turned[a][:, u, :], z[:, cols], ident[:])
 
-        def regroup(a, lo, hi):
-            source = turned[a][:].rearrange("j u (q e b) -> j e (u q) b", e=2, b=2)
-            nc.vector.tensor_copy(z_rows[a][:, :, lo:hi, :], source[:, :, lo:hi, :])
+        def gate(u, a, ub, sg):
+            cols = slice(a * P, (a + 1) * P)
+            nc.vector.scalar_tensor_tensor(
+                z_half[a][:, :, u, :], ub[:, cols].rearrange("p (b j) -> p b j", b=2), gain[:, u:u + 1],
+                sg[:, cols].rearrange("p (b j) -> p b j", b=2), ALU.mult, ALU.mult)
 
         ranked_a = rank(0, [fetch_pair(u, acc[u]) for u in range(2)])
 
@@ -186,14 +192,13 @@ def tile_picked_mtthzceordcpsw_none_po_kernel(
         for name, source in (("n6", n6), ("n7", n7), ("n8", n8), ("n9", n9), ("n10", n10)):
             L[name] = load_list(name, source)
 
-        sg0 = tile("sg0", [P, S], F32)
-        z0 = tile("z0", [P, S], F32, tag="pair1")
-        sg1 = tile("sg1", [P, S], F32, tag="h2")
-        z1 = tile("z1", [P, S], F32)
-        for a in range(2):
-            gate(0, a, ub0, sg0, z0)
-        for a in range(2):
-            gate(1, a, ub1, sg1, z1)
+        z_half[0] = tile("z_half0", [P, 2, 4, 64], BF16, tag="pair1")
+        z_half[1] = tile("z_half1", [P, 2, 4, 64], BF16, tag="planes_b")
+        for u, ub, tag in ((0, ub0, None), (1, ub1, "h2")):
+            sg = tile(f"sg{u}", [P, S], F32, tag=tag)
+            squash(u, ub, sg, 0, S)
+            for a in range(2):
+                gate(u, a, ub, sg)
 
         c_pick = tile("c_pick", [P, 4, P], U32, tag="pair3")
         for half in range(2):
@@ -201,28 +206,28 @@ def tile_picked_mtthzceordcpsw_none_po_kernel(
                                   x_tab[:].indirect(part("cand", half)))
 
         ub2, ub3 = put_back(2, *ranked_b)
-        late = [(u, ub, tile(f"sg{u}", [P, S], F32), tile(f"z{u}", [P, S], F32)) for u, ub in ((2, ub2), (3, ub3))]
+        late = [(u, ub, tile(f"sg{u}", [P, S], F32)) for u, ub in ((2, ub2), (3, ub3))]
         for a in range(2):
-            for u, ub, sg, z in late:
-                gate(u, a, ub, sg, z)
-                if u == 2:
-                    regroup(a, 0, 96)
-                else:
-                    regroup(a, 96, 128)
+            for u, ub, sg in late:
+                squash(u, ub, sg, a * P, (a + 1) * P)
+                gate(u, a, ub, sg)
 
         z_codes = tile("z_codes", [P, S], U32)
         z_scales = tile("z_scales", [P, S], U8)
         s_acc = [psum.tile([P, S], F32, name=f"s_acc{t}", tag=f"acc{t}") for t in range(4)]
-        scores = [tile(f"scores{t}", [P, S], F32) for t in range(4)]
         for a in range(2):
             cols = slice(a * P, (a + 1) * P)
-            back = psum.tile([P, 2, P], F32, name=f"back{a}", tag=f"back{a}")
-            pairs = z_rows[a][:].rearrange("j e p b -> j (e p b)").bitcast(F32)
-            for e in range(2):
-                nc.tensor.transpose(back[:, e, :], pairs[:, e * P:(e + 1) * P], ident[:])
+            dealt = tile(f"dealt{a}", [P, 2, P], F32)
+            for b in range(2):
+                turned = psum.tile([P, P], F32, name=f"turned{a}_{b}", tag=f"turned{a}_{b}")
+                pairs = z_half[a][:].rearrange("m b u j -> m (b u j)").bitcast(F32)[:, b * P:(b + 1) * P]
+                nc.tensor.transpose(turned[:].rearrange("w (t q) -> w t q", t=4), pairs,
+                                    ident[:].rearrange("m (q t) -> m t q", t=4))
+                nc.vector.transpose(dealt[:, b, :], turned[:])
             z_bf = tile(f"z_bf{a}", [P, 4 * P], BF16)
-            nc.vector.tensor_copy(z_bf[:].bitcast(F32).rearrange("p (j e) -> p j e", e=2),
-                                  back[:].rearrange("p e j -> p j e"))
+            nc.vector.tensor_copy(
+                z_bf[:].rearrange("p (b j t) -> p b j t", b=2, t=4),
+                dealt[:].rearrange("p b w -> p (b w)").bitcast(BF16).rearrange("p (b t j) -> p b j t", b=2, t=4))
             nc.vector.quantize_mx(out=z_codes[:, cols].bitcast(FP8X4), scales=z_scales[:, cols], in_=z_bf[:])
             for t in range(4):
                 nc.tensor.matmul_mx(
@@ -234,7 +239,7 @@ def tile_picked_mtthzceordcpsw_none_po_kernel(
             else:
                 nc.scalar.activation(scores[0][:, cols], s_acc[0][:, cols], ACT.Copy, scale=SIXTEENTH)
         for t in range(1, 4):
-            nc.vector.tensor_scalar(scores[t][:], s_acc[t][:], SIXTEENTH, None, ALU.mult)
+            nc.vector.tensor_scalar(scores[t][:, :S], s_acc[t][:], SIXTEENTH, None, ALU.mult)
 
         result = tile("result", [P, 4, S], F32)
         rows = out_0.rearrange("(p t) j -> p t j", t=4)
@@ -249,22 +254,20 @@ def tile_picked_mtthzceordcpsw_none_po_kernel(
             nc.scalar.activation(placed[:].indirect(L["n9"][:]), larger[:], ACT.Copy)
             return placed
 
-        def subtract(t, placed):
+        def subtract(t, placed, pieces):
             other = tile(f"other{t}", [P, S], F32, tag="larger3" if t == 3 else None)
-            for a in range(2):
-                cols = slice(a * P, (a + 1) * P)
-                nc.scalar.activation(other[:, cols], scores[t][:].indirect(L["n10"][:, 8 * a:8 * (a + 1)]), ACT.Copy)
+            width = S // pieces
+            for lo in range(0, S, width):
+                cols = slice(lo, lo + width)
+                nc.scalar.activation(other[:, cols], scores[t][:].indirect(L["n10"][:, lo // 16:(lo + width) // 16]), ACT.Copy)
                 nc.vector.tensor_tensor(result[:, t, cols], placed[:, cols], other[:, cols], ALU.subtract)
-                if t == 3:
-                    nc.sync.dma_start(rows[:, t, cols], result[:, t, cols])
-            if t < 3:
-                nc.sync.dma_start(rows[:, t, :], result[:, t, :])
+                nc.sync.dma_start(rows[:, t, cols], result[:, t, cols])
 
         placed = [place(0)]
         for t in range(1, 4):
             placed.append(place(t))
-            subtract(t - 1, placed[t - 1])
-        subtract(3, placed[3])
+            subtract(t - 1, placed[t - 1], 1)
+        subtract(3, placed[3], 2)
 
         y_codes = tile("y_codes", [P, S], U32)
         y_scales = tile("y_scales", [P, S], U8)

@@ -17,7 +17,11 @@ ALU = mybir.AluOpType
 ACT = mybir.ActivationFunctionType
 
 P = 128
-HALF = 256
+PACK = 4
+LIST_HALF = H // 2
+STRIPE = 16
+RUN = 64
+SPARE = 32
 SIXTEENTH = 0.0625
 
 
@@ -27,129 +31,138 @@ def tile_picked_mtthzceordcpsw_none_po_kernel(
 ):
     nc = tc.nc
     with ExitStack() as ctx:
-        lists = ctx.enter_context(tc.tile_pool(name="lists", bufs=1))
+        list_pool = ctx.enter_context(tc.tile_pool(name="lists", bufs=1))
         sb = ctx.enter_context(tc.tile_pool(name="sb", bufs=1))
         psum = ctx.enter_context(tc.psum_pool(name="psum", bufs=1))
+        lists = {}
 
-        def tile(name, shape, dtype, tag=None):
-            return sb.tile(shape, dtype, name=name, tag=tag or name, align_bytes=64)
+        def tile(name, shape, dtype, after=None):
+            return sb.tile(shape, dtype, name=name, tag=after or name, align_bytes=64)
 
-        def load_list(name, source):
-            held = lists.tile(list(source.shape), U16, name=name, tag=name)
-            nc.sync.dma_start(held[:], source)
-            return held
+        def load_lists(*named):
+            for name, source in named:
+                lists[name] = list_pool.tile(list(source.shape), U16, name=name, tag=name)
+                nc.sync.dma_start(lists[name][:], source)
+
+        def entries(name, lo, hi):
+            return lists[name][:, lo // STRIPE:hi // STRIPE]
 
         d_bytes = tile("d_bytes", [P, G], U8)
         x_bytes = tile("x_bytes", [P, T], U8)
-        nc.gpsimd.memset(d_bytes[:].bitcast(I32), 0)
         nc.vector.memset(x_bytes[:].bitcast(I32), 0)
+        nc.vector.memset(d_bytes[:].bitcast(I32), 0)
         nc.sync.dma_start(x_bytes[:].bitcast(I32)[0:P:8, :], x_scales[0].bitcast(I32))
+
         warm_in = tile("warm_in", [P, 1], F32)
         warm_out = tile("warm_out", [P, 1], F32)
         nc.vector.memset(warm_in[:], 0.0)
         nc.scalar.activation(warm_out[:], warm_in[:], ACT.Sigmoid)
-        L = {}
-        for name, source in (("hz", hz), ("offs", offs), ("two", two)):
-            L[name] = load_list(name, source)
-        nc.sync.dma_start(d_bytes[:].bitcast(I32)[0:P:8, :], d_scales[0].bitcast(I32))
-        for name, source in (("k1", k1), ("k2", k2), ("k3", k3)):
-            L[name] = load_list(name, source)
-        x_tab = tile("x_tab", [P, T], U32)
-        d_tab = tile("d_tab", [P, G], U32)
-        nc.sync.dma_start(x_tab[:].bitcast(I32), x_words[0].rearrange("p n t -> p (n t)").bitcast(I32))
-        d_source = d_words[0].rearrange("p n t -> p (n t)").bitcast(I32)
-        nc.gpsimd.dma_start(d_tab[:].bitcast(I32)[:, :G // 2], d_source[:, :G // 2])
-        nc.sync.dma_start(d_tab[:].bitcast(I32)[:, G // 2:], d_source[:, G // 2:])
 
-        wide_ub = [tile(f"ub{u}", [P, 2 * S], F32) for u in range(2)]
-        scores = [tile(f"scores{t}", [P, S + 32 if t < 3 else S], F32) for t in range(4)]
-        for window in wide_ub + scores[:3]:
+        load_lists(("hz", hz), ("offs", offs), ("two", two))
+        nc.sync.dma_start(d_bytes[:].bitcast(I32)[0:P:8, :], d_scales[0].bitcast(I32))
+        load_lists(("k1", k1), ("k2", k2), ("k3", k3))
+        x_table = tile("x_table", [P, T], U32)
+        d_table = tile("d_table", [P, G], U32)
+        nc.sync.dma_start(x_table[:].bitcast(I32), x_words[0].rearrange("p n t -> p (n t)").bitcast(I32))
+        d_source = d_words[0].rearrange("p n t -> p (n t)").bitcast(I32)
+        nc.gpsimd.dma_start(d_table[:].bitcast(I32)[:, :G // 2], d_source[:, :G // 2])
+        nc.sync.dma_start(d_table[:].bitcast(I32)[:, G // 2:], d_source[:, G // 2:])
+
+        ub = [tile(f"ub{u}", [P, 2 * S if u < 2 else S], F32) for u in range(PACK)]
+        scores = [tile(f"scores{t}", [P, S + SPARE if t < 2 else S], F32) for t in range(PACK)]
+        for window in ub[:2] + scores[:2]:
             nc.gpsimd.memset(window[:, S:], 0.0)
-        slope = tile("slope", [P, 4], F32)
-        thresh = tile("thresh", [P, 4], F32)
-        gain = tile("gain", [P, 4], F32)
+
+        slope = tile("slope", [P, PACK], F32)
+        thresh = tile("thresh", [P, PACK], F32)
+        gain = tile("gain", [P, PACK], F32)
         with nc.allow_non_contiguous_dma(reason="one float32 value a row"):
             for held, source in ((slope, sl), (thresh, th), (gain, gs)):
                 nc.gpsimd.dma_start(held[:], source.rearrange("(u p) o -> p (u o)", p=P))
-        slope_thresh = tile("slope_thresh", [P, 4], F32)
-        bias = tile("bias", [P, 4], F32)
+        slope_thresh = tile("slope_thresh", [P, PACK], F32)
+        bias = tile("bias", [P, PACK], F32)
         nc.gpsimd.tensor_tensor(slope_thresh[:], slope[:], thresh[:], ALU.mult)
         nc.gpsimd.tensor_scalar(bias[:], slope_thresh[:], -1.0, 0.0, ALU.mult, ALU.add)
         ident = tile("ident", [P, P], F32)
         make_identity(nc, ident[:])
 
-        planes_a = tile("planes_a", [P, 6 * HALF], U8)
-        planes_b = tile("planes_b", [P, 3 * HALF], U8)
-        planes_c = tile("planes_c", [P, C], U8)
-        for plane in (planes_a, planes_b, planes_c):
-            nc.vector.memset(plane[:].bitcast(I32), 0)
+        planes_first = tile("planes_first", [P, 3 * LIST_HALF + 3 * S], U8)
+        planes_second = tile("planes_second", [P, 3 * LIST_HALF], U8)
+        planes_cand = tile("planes_cand", [P, C], U8)
+        for planes in (planes_first, planes_second, planes_cand):
+            nc.vector.memset(planes[:].bitcast(I32), 0)
 
-        def seat_rows(queues, plane, picked):
+        def seat_rows(queues, planes, picked):
             for s in range(4):
-                queues[s % 2].dma_start(plane[:].bitcast(I32)[s:P:32, :], picked[:].bitcast(I32)[8 * s:P:32, :])
-
-        def part(name, half):
-            return L[name][:, 16 * half:16 * (half + 1)]
+                queues[s % len(queues)].dma_start(planes.bitcast(I32)[s:P:32, :], picked.bitcast(I32)[8 * s:P:32, :])
 
         d_names = ("k1", "k2", "k3")
         x_names = ("offs", "two", "hz")
 
-        picked_a = tile("picked_a", [P, 6 * HALF], U8, tag="picked")
-        for g in (2, 0, 1):
-            nc.vector.tensor_copy(picked_a[:, (3 + g) * HALF:(4 + g) * HALF], x_bytes[:].indirect(L[x_names[g]][:]))
-        for g, name in enumerate(d_names):
-            nc.vector.tensor_copy(picked_a[:, g * HALF:(g + 1) * HALF], d_bytes[:].indirect(part(name, 0)))
-        seat_rows((nc.scalar, nc.sync), planes_a, picked_a)
-        for name, source in (("n1", n1), ("n2", n2), ("n3", n3), ("n4", n4), ("n5", n5), ("cand", cand)):
-            L[name] = load_list(name, source)
-        x_pick = []
-        for name in x_names:
-            words = tile("xw_" + name, [P, S], U32)
-            nc.vector.tensor_copy(words[:], x_tab[:].indirect(L[name][:]))
-            x_pick.append(words)
+        def d_cols(g):
+            return slice(g * LIST_HALF, (g + 1) * LIST_HALF)
 
-        def first_product(d_pick, planes, acc):
-            for v in range(2):
-                for g in range(3):
-                    cols = slice(g * HALF + v * P, g * HALF + (v + 1) * P)
-                    nc.tensor.matmul_mx(
-                        out=acc[v][:], lhsT=d_pick[g][:, v * P:(v + 1) * P].bitcast(FP8X4), lhsT_scale=planes[:, cols],
-                        rhs=x_pick[g][:].bitcast(FP8X4), rhs_scale=planes_a[:, (3 + g) * HALF:(4 + g) * HALF],
-                        start=(g == 0), stop=(g == 2))
+        def x_cols(g):
+            return slice(3 * LIST_HALF + g * S, 3 * LIST_HALF + (g + 1) * S)
 
-        def pick_words(half, tags):
+        def pick_d_bytes(half, picked):
+            for g, name in enumerate(d_names):
+                offsets = entries(name, half * LIST_HALF, (half + 1) * LIST_HALF)
+                nc.vector.tensor_copy(picked[:, d_cols(g)], d_bytes[:].indirect(offsets))
+
+        def pick_d_words(half, afters):
             picked = []
-            for name, tag in zip(d_names, tags):
-                words = tile(f"dw_{name}_{half}", [P, HALF], U32, tag=tag)
-                nc.vector.tensor_copy(words[:], d_tab[:].indirect(part(name, half)))
+            for name, after in zip(d_names, afters):
+                words = tile(f"d_words_{name}_{half}", [P, LIST_HALF], U32, after=after)
+                offsets = entries(name, half * LIST_HALF, (half + 1) * LIST_HALF)
+                nc.vector.tensor_copy(words[:], d_table[:].indirect(offsets))
                 picked.append(words)
             return picked
 
-        d_pick_a = pick_words(0, (None, None, None))
-        acc = [psum.tile([P, S], F32, name=f"h_acc{u}", tag=f"acc{u}") for u in range(2)]
-        first_product(d_pick_a, planes_a, acc)
+        def first_products(half, d_picked, d_planes):
+            sums = [psum.tile([P, S], F32, name=f"h_sum{u}", tag=f"bank{u}") for u in (2 * half, 2 * half + 1)]
+            for v in range(2):
+                for g in range(3):
+                    nc.tensor.matmul_mx(
+                        out=sums[v][:],
+                        lhsT=d_picked[g][:, v * P:(v + 1) * P].bitcast(FP8X4),
+                        lhsT_scale=d_planes[:, g * LIST_HALF + v * P:g * LIST_HALF + (v + 1) * P],
+                        rhs=x_picked[g][:].bitcast(FP8X4),
+                        rhs_scale=planes_first[:, x_cols(g)],
+                        start=(g == 0), stop=(g == 2))
+            return sums
 
-        picked_b = tile("picked_b", [P, 3 * HALF], U8, tag="picked")
-        for g, name in enumerate(d_names):
-            nc.vector.tensor_copy(picked_b[:, g * HALF:(g + 1) * HALF], d_bytes[:].indirect(part(name, 1)))
-        seat_rows((nc.sync, nc.sync), planes_b, picked_b)
+        bytes_first = tile("bytes_first", [P, 3 * LIST_HALF + 3 * S], U8)
+        for name in ("hz", "offs", "two"):
+            nc.vector.tensor_copy(bytes_first[:, x_cols(x_names.index(name))], x_bytes[:].indirect(lists[name][:]))
+        pick_d_bytes(0, bytes_first)
+        seat_rows((nc.scalar, nc.sync), planes_first[:], bytes_first[:])
+        load_lists(("n1", n1), ("n2", n2), ("n3", n3), ("n4", n4), ("n5", n5), ("cand", cand))
+        x_picked = []
+        for name in x_names:
+            words = tile("x_words_" + name, [P, S], U32)
+            nc.vector.tensor_copy(words[:], x_table[:].indirect(lists[name][:]))
+            x_picked.append(words)
+        sums_first = first_products(0, pick_d_words(0, (None, None, None)), planes_first)
 
-        z_half = [None, None]
+        bytes_second = tile("bytes_second", [P, 3 * LIST_HALF], U8, after="bytes_first")
+        pick_d_bytes(1, bytes_second)
+        seat_rows((nc.sync,), planes_second[:], bytes_second[:])
 
-        def fetch_pair(u, source):
+        def fetch_pair(u, h_sum):
             h = tile(f"h{u}", [P, S], F32)
-            if u < 2:
-                nc.scalar.activation(h[:], source[:], ACT.Copy, scale=SIXTEENTH)
+            if u == 0:
+                nc.scalar.activation(h[:], h_sum[:], ACT.Copy, scale=SIXTEENTH)
             else:
-                nc.vector.tensor_scalar(h[:], source[:], SIXTEENTH, None, ALU.mult)
+                nc.vector.tensor_scalar(h[:], h_sum[:], SIXTEENTH, None, ALU.mult)
             pair = tile(f"pair{u}", [P, 2, W], F32)
-            nc.scalar.activation(pair[:, 0, :], h[:].indirect(L["n1"][:]), ACT.Copy)
-            nc.scalar.activation(pair[:, 1, :], h[:].indirect(L["n2"][:]), ACT.Copy)
+            nc.scalar.activation(pair[:, 0, :], h[:].indirect(lists["n1"][:]), ACT.Copy)
+            nc.scalar.activation(pair[:, 1, :], h[:].indirect(lists["n2"][:]), ACT.Copy)
             return pair
 
         def rank(u, pairs):
             high = [tile(f"high{u + v}", [P, W], F32) for v in range(2)]
-            low = [tile(f"low{u}", [P, W], F32, tag=f"h{u + 1}"), tile(f"low{u + 1}", [P, W], F32)]
+            low = [tile(f"low{u}", [P, W], F32, after=f"h{u + 1}"), tile(f"low{u + 1}", [P, W], F32)]
             for v in range(2):
                 nc.vector.tensor_tensor(high[v][:], pairs[v][:, 0, :], pairs[v][:, 1, :], ALU.max)
             for v in range(2):
@@ -157,127 +170,123 @@ def tile_picked_mtthzceordcpsw_none_po_kernel(
             return high, low
 
         def put_back(u, high, low):
-            ub = wide_ub if u == 0 else [tile(f"ub{u + v}", [P, S], F32) for v in range(2)]
             for v in range(2):
-                nc.scalar.activation(ub[v][:].indirect(L["n3"][:]), high[v][:], ACT.Copy)
+                nc.scalar.activation(ub[u + v][:].indirect(lists["n3"][:]), high[v][:], ACT.Copy)
             for v in range(2):
-                nc.scalar.activation(ub[v][:].indirect(L["n4"][:]), low[v][:], ACT.Copy)
-            return ub
+                nc.scalar.activation(ub[u + v][:].indirect(lists["n4"][:]), low[v][:], ACT.Copy)
 
-        def squash(u, ub, sg, lo, hi):
-            nc.scalar.activation(sg[:, lo:hi], ub[:].indirect(L["n5"][:, lo // 16:hi // 16]), ACT.Sigmoid,
+        def fetch_sigmoid(u, sg, lo, hi):
+            nc.scalar.activation(sg[:, lo:hi], ub[u][:].indirect(entries("n5", lo, hi)), ACT.Sigmoid,
                                  bias=bias[:, u:u + 1], scale=slope[:, u:u + 1])
 
-        def gate(u, a, ub, sg):
+        def gate(u, a, sg, z_half):
             cols = slice(a * P, (a + 1) * P)
             nc.vector.scalar_tensor_tensor(
-                z_half[a][:, :, u, :], ub[:, cols].rearrange("p (b j) -> p b j", b=2), gain[:, u:u + 1],
-                sg[:, cols].rearrange("p (b j) -> p b j", b=2), ALU.mult, ALU.mult)
+                z_half[:, :, u, :], ub[u][:, cols].rearrange("p (b j) -> p b j", j=RUN), gain[:, u:u + 1],
+                sg[:, cols].rearrange("p (b j) -> p b j", j=RUN), ALU.mult, ALU.mult)
 
-        ranked_a = rank(0, [fetch_pair(u, acc[u]) for u in range(2)])
+        ranked_first = rank(0, [fetch_pair(u, sums_first[u]) for u in range(2)])
 
-        d_pick_b = pick_words(1, ("h0", "pair0", "pair1"))
-        acc_b = [psum.tile([P, S], F32, name=f"h_acc{u}", tag=f"acc{u}") for u in range(2, 4)]
-        first_product(d_pick_b, planes_b, acc_b)
+        sums_second = first_products(1, pick_d_words(1, ("h0", "pair0", "pair1")), planes_second)
+        put_back(0, *ranked_first)
+        ranked_second = rank(2, [fetch_pair(2 + v, sums_second[v]) for v in range(2)])
 
-        ub0, ub1 = put_back(0, *ranked_a)
+        bytes_cand = tile("bytes_cand", [P, PACK, P], U8, after="pair2")
+        nc.vector.tensor_copy(bytes_cand[:].rearrange("p t m -> p m t"), x_bytes[:].indirect(lists["cand"][:]))
+        seat_rows((nc.sync,), planes_cand[:], bytes_cand[:].rearrange("p t m -> p (t m)"))
+        load_lists(("n6", n6), ("n7", n7), ("n8", n8), ("n9", n9), ("n10", n10))
 
-        ranked_b = rank(2, [fetch_pair(2 + v, acc_b[v]) for v in range(2)])
-
-        picked_c = tile("picked_c", [P, 4, P], U8, tag="pair2")
-        nc.vector.tensor_copy(picked_c[:].rearrange("p t m -> p m t"), x_bytes[:].indirect(L["cand"][:]))
-        for s in range(4):
-            nc.sync.dma_start(planes_c[:].bitcast(I32)[s:P:32, :],
-                              picked_c[:].rearrange("p t m -> p (t m)").bitcast(I32)[8 * s:P:32, :])
-        for name, source in (("n6", n6), ("n7", n7), ("n8", n8), ("n9", n9), ("n10", n10)):
-            L[name] = load_list(name, source)
-
-        z_half[0] = tile("z_half0", [P, 2, 4, 64], BF16, tag="pair1")
-        z_half[1] = tile("z_half1", [P, 2, 4, 64], BF16, tag="planes_b")
-        for u, ub, tag in ((0, ub0, None), (1, ub1, "h2")):
-            sg = tile(f"sg{u}", [P, S], F32, tag=tag)
-            squash(u, ub, sg, 0, S)
+        z_halves = [tile("z_half0", [P, 2, PACK, RUN], BF16, after="pair1"),
+                    tile("z_half1", [P, 2, PACK, RUN], BF16, after="planes_second")]
+        for u, after in ((0, None), (1, "h2")):
+            sg = tile(f"sg{u}", [P, S], F32, after=after)
+            fetch_sigmoid(u, sg, 0, S)
             for a in range(2):
-                gate(u, a, ub, sg)
+                gate(u, a, sg, z_halves[a])
 
-        c_pick = tile("c_pick", [P, 4, P], U32, tag="pair3")
+        words_cand = tile("words_cand", [P, PACK, P], U32, after="pair3")
         for half in range(2):
-            nc.vector.tensor_copy(c_pick[:].rearrange("p t m -> p m t")[:, 64 * half:64 * (half + 1), :],
-                                  x_tab[:].indirect(part("cand", half)))
+            nc.vector.tensor_copy(words_cand[:].rearrange("p t m -> p m t")[:, half * P // 2:(half + 1) * P // 2, :],
+                                  x_table[:].indirect(entries("cand", half * C // 2, (half + 1) * C // 2)))
 
-        ub2, ub3 = put_back(2, *ranked_b)
-        late = [(u, ub, tile(f"sg{u}", [P, S], F32)) for u, ub in ((2, ub2), (3, ub3))]
+        put_back(2, *ranked_second)
+        late_sg = {u: tile(f"sg{u}", [P, S], F32) for u in (2, 3)}
         for a in range(2):
-            for u, ub, sg in late:
-                squash(u, ub, sg, a * P, (a + 1) * P)
-                gate(u, a, ub, sg)
+            for u in (2, 3):
+                fetch_sigmoid(u, late_sg[u], a * P, (a + 1) * P)
+                gate(u, a, late_sg[u], z_halves[a])
 
         z_codes = tile("z_codes", [P, S], U32)
         z_scales = tile("z_scales", [P, S], U8)
-        s_acc = [psum.tile([P, S], F32, name=f"s_acc{t}", tag=f"acc{t}") for t in range(4)]
+        s_sums = [psum.tile([P, S], F32, name=f"s_sum{t}", tag=f"bank{t}") for t in range(PACK)]
         for a in range(2):
             cols = slice(a * P, (a + 1) * P)
             dealt = tile(f"dealt{a}", [P, 2, P], F32)
             for b in range(2):
                 turned = psum.tile([P, P], F32, name=f"turned{a}_{b}", tag=f"turned{a}_{b}")
-                pairs = z_half[a][:].rearrange("m b u j -> m (b u j)").bitcast(F32)[:, b * P:(b + 1) * P]
-                nc.tensor.transpose(turned[:].rearrange("w (t q) -> w t q", t=4), pairs,
-                                    ident[:].rearrange("m (q t) -> m t q", t=4))
+                z_words = z_halves[a][:].rearrange("m b u j -> m (b u j)").bitcast(F32)[:, b * P:(b + 1) * P]
+                nc.tensor.transpose(turned[:].rearrange("w (t q) -> w t q", t=PACK), z_words,
+                                    ident[:].rearrange("m (q t) -> m t q", t=PACK))
                 nc.vector.transpose(dealt[:, b, :], turned[:])
-            z_bf = tile(f"z_bf{a}", [P, 4 * P], BF16)
+            z_woven = tile(f"z_woven{a}", [P, PACK * P], BF16)
             nc.vector.tensor_copy(
-                z_bf[:].rearrange("p (b j t) -> p b j t", b=2, t=4),
-                dealt[:].rearrange("p b w -> p (b w)").bitcast(BF16).rearrange("p (b t j) -> p b j t", b=2, t=4))
-            nc.vector.quantize_mx(out=z_codes[:, cols].bitcast(FP8X4), scales=z_scales[:, cols], in_=z_bf[:])
-            for t in range(4):
+                z_woven[:].rearrange("p (b j t) -> p b j t", b=2, t=PACK),
+                dealt[:].rearrange("p b w -> p (b w)").bitcast(BF16).rearrange("p (b t j) -> p b j t", b=2, t=PACK))
+            nc.vector.quantize_mx(out=z_codes[:, cols].bitcast(FP8X4), scales=z_scales[:, cols], in_=z_woven[:])
+            for t in range(PACK):
                 nc.tensor.matmul_mx(
-                    out=s_acc[t][:, cols], lhsT=c_pick[:, t, :].bitcast(FP8X4),
-                    lhsT_scale=planes_c[:, t * P:(t + 1) * P],
+                    out=s_sums[t][:, cols],
+                    lhsT=words_cand[:, t, :].bitcast(FP8X4), lhsT_scale=planes_cand[:, t * P:(t + 1) * P],
                     rhs=z_codes[:, cols].bitcast(FP8X4), rhs_scale=z_scales[:, cols], start=True, stop=True)
             if a == 0:
-                nc.vector.tensor_scalar(scores[0][:, cols], s_acc[0][:, cols], SIXTEENTH, None, ALU.mult)
+                nc.vector.tensor_scalar(scores[0][:, cols], s_sums[0][:, cols], SIXTEENTH, None, ALU.mult)
             else:
-                nc.scalar.activation(scores[0][:, cols], s_acc[0][:, cols], ACT.Copy, scale=SIXTEENTH)
-        for t in range(1, 4):
-            nc.vector.tensor_scalar(scores[t][:, :S], s_acc[t][:], SIXTEENTH, None, ALU.mult)
+                nc.scalar.activation(scores[0][:, cols], s_sums[0][:, cols], ACT.Copy, scale=SIXTEENTH)
+        for t in range(1, PACK):
+            nc.vector.tensor_scalar(scores[t][:, :S], s_sums[t][:], SIXTEENTH, None, ALU.mult)
 
-        result = tile("result", [P, 4, S], F32)
-        rows = out_0.rearrange("(p t) j -> p t j", t=4)
+        result = tile("result", [P, PACK, S], F32)
+        out_rows = out_0.rearrange("(p t) j -> p t j", t=PACK)
+
         def place(t):
             pair = tile(f"s_pair{t}", [P, 2, W], F32)
-            nc.scalar.activation(pair[:, 0, :], scores[t][:].indirect(L["n6"][:]), ACT.Copy)
-            nc.scalar.activation(pair[:, 1, :], scores[t][:].indirect(L["n7"][:]), ACT.Copy)
+            nc.scalar.activation(pair[:, 0, :], scores[t][:].indirect(lists["n6"][:]), ACT.Copy)
+            nc.scalar.activation(pair[:, 1, :], scores[t][:].indirect(lists["n7"][:]), ACT.Copy)
             larger = tile(f"larger{t}", [P, W], F32)
             nc.vector.tensor_tensor(larger[:], pair[:, 0, :], pair[:, 1, :], ALU.max)
-            placed = tile(f"placed{t}", [P, S], F32)
-            nc.scalar.activation(placed[:].indirect(L["n8"][:]), pair[:, 1, :], ACT.Copy)
-            nc.scalar.activation(placed[:].indirect(L["n9"][:]), larger[:], ACT.Copy)
-            return placed
+            ub2 = tile(f"ub2_{t}", [P, S], F32)
+            nc.scalar.activation(ub2[:].indirect(lists["n8"][:]), pair[:, 1, :], ACT.Copy)
+            nc.scalar.activation(ub2[:].indirect(lists["n9"][:]), larger[:], ACT.Copy)
+            return ub2
 
-        def subtract(t, placed, pieces):
-            other = tile(f"other{t}", [P, S], F32, tag="larger3" if t == 3 else None)
-            width = S // pieces
+        def subtract(t, ub2, after=None):
+            other = tile(f"other{t}", [P, S], F32, after=after)
+            width = S if t < 2 else S // 2
             for lo in range(0, S, width):
                 cols = slice(lo, lo + width)
-                nc.scalar.activation(other[:, cols], scores[t][:].indirect(L["n10"][:, lo // 16:(lo + width) // 16]), ACT.Copy)
-                nc.vector.tensor_tensor(result[:, t, cols], placed[:, cols], other[:, cols], ALU.subtract)
-                nc.sync.dma_start(rows[:, t, cols], result[:, t, cols])
+                nc.scalar.activation(other[:, cols], scores[t][:].indirect(entries("n10", lo, lo + width)), ACT.Copy)
+                nc.vector.tensor_tensor(result[:, t, cols], ub2[:, cols], other[:, cols], ALU.subtract)
+                nc.sync.dma_start(out_rows[:, t, cols], result[:, t, cols])
 
         placed = [place(0)]
-        for t in range(1, 4):
+        for t in range(1, PACK):
             placed.append(place(t))
-            subtract(t - 1, placed[t - 1], 1)
-        subtract(3, placed[3], 2)
+            subtract(t - 1, placed[t - 1])
+        last = PACK - 1
+        y_woven = [tile(f"y_woven{a}", [P, P, PACK], BF16) for a in range(2)]
+        for a in range(2):
+            nc.vector.tensor_copy(y_woven[a][:, :, :last],
+                                  result[:, :last, a * P:(a + 1) * P].rearrange("p t j -> p j t"))
+        subtract(last, placed[last], after=f"s_pair{last}")
 
         y_codes = tile("y_codes", [P, S], U32)
         y_scales = tile("y_scales", [P, S], U8)
         codes_out = out_1[0].rearrange("p n t -> p (n t)").bitcast(I32)
         for a in range(2):
             cols = slice(a * P, (a + 1) * P)
-            y_bf = tile(f"y_bf{a}", [P, P, 4], BF16)
-            nc.vector.tensor_copy(y_bf[:], result[:, :, cols].rearrange("p t j -> p j t"))
+            nc.vector.tensor_copy(y_woven[a][:, :, last], result[:, last, cols])
             nc.vector.quantize_mx(out=y_codes[:, cols].bitcast(FP8X4), scales=y_scales[:, cols],
-                                  in_=y_bf[:].rearrange("p j t -> p (j t)"))
+                                  in_=y_woven[a][:].rearrange("p j t -> p (j t)"))
             nc.sync.dma_start(codes_out[:, cols], y_codes[:, cols].bitcast(I32))
         for q in range(4):
             queue = nc.sync if q % 2 else nc.scalar

from contextlib import ExitStack

import concourse.mybir as mybir
from concourse.masks import make_identity

K, T, S, G, H, W, C = 512, 1024, 256, 2048, 512, 128, 512
FLOPS = 2 * K * S * (3 * H + C)

F32 = mybir.dt.float32
BF16 = mybir.dt.bfloat16
I32 = mybir.dt.int32
U32 = mybir.dt.uint32
U16 = mybir.dt.uint16
U8 = mybir.dt.uint8
FP8X4 = mybir.dt.float8_e4m3fn_x4
ALU = mybir.AluOpType
ACT = mybir.ActivationFunctionType

P = 128
PACK = 4
LIST_HALF = H // 2
STRIPE = 16
RUN = 64
SPARE = 32
SIXTEENTH = 0.0625


def tile_picked_mtthzceordcpsw_none_po_kernel(
    tc, x_words, x_scales, d_words, d_scales, sl, th, gs, offs, k1, two, k2, hz, k3,
    n1, n2, n3, n4, n5, cand, n6, n7, n8, n9, n10, out_0, out_1, out_2,
):
    nc = tc.nc
    with ExitStack() as ctx:
        list_pool = ctx.enter_context(tc.tile_pool(name="lists", bufs=1))
        sb = ctx.enter_context(tc.tile_pool(name="sb", bufs=1))
        psum = ctx.enter_context(tc.psum_pool(name="psum", bufs=1))
        lists = {}

        def tile(name, shape, dtype, after=None):
            return sb.tile(shape, dtype, name=name, tag=after or name, align_bytes=64)

        def load_lists(*named):
            for name, source in named:
                lists[name] = list_pool.tile(list(source.shape), U16, name=name, tag=name)
                nc.sync.dma_start(lists[name][:], source)

        def entries(name, lo, hi):
            return lists[name][:, lo // STRIPE:hi // STRIPE]

        d_bytes = tile("d_bytes", [P, G], U8)
        x_bytes = tile("x_bytes", [P, T], U8)
        nc.vector.memset(x_bytes[:].bitcast(I32), 0)
        nc.vector.memset(d_bytes[:].bitcast(I32), 0)
        nc.sync.dma_start(x_bytes[:].bitcast(I32)[0:P:8, :], x_scales[0].bitcast(I32))

        warm_in = tile("warm_in", [P, 1], F32)
        warm_out = tile("warm_out", [P, 1], F32)
        nc.vector.memset(warm_in[:], 0.0)
        nc.scalar.activation(warm_out[:], warm_in[:], ACT.Sigmoid)

        load_lists(("hz", hz), ("offs", offs), ("two", two))
        nc.sync.dma_start(d_bytes[:].bitcast(I32)[0:P:8, :], d_scales[0].bitcast(I32))
        load_lists(("k1", k1), ("k2", k2), ("k3", k3))
        x_table = tile("x_table", [P, T], U32)
        d_table = tile("d_table", [P, G], U32)
        nc.sync.dma_start(x_table[:].bitcast(I32), x_words[0].rearrange("p n t -> p (n t)").bitcast(I32))
        d_source = d_words[0].rearrange("p n t -> p (n t)").bitcast(I32)
        nc.gpsimd.dma_start(d_table[:].bitcast(I32)[:, :G // 2], d_source[:, :G // 2])
        nc.sync.dma_start(d_table[:].bitcast(I32)[:, G // 2:], d_source[:, G // 2:])

        ub = [tile(f"ub{u}", [P, 2 * S if u < 2 else S], F32) for u in range(PACK)]
        scores = [tile(f"scores{t}", [P, S + SPARE if t < 2 else S], F32) for t in range(PACK)]
        for window in ub[:2] + scores[:2]:
            nc.gpsimd.memset(window[:, S:], 0.0)

        slope = tile("slope", [P, PACK], F32)
        thresh = tile("thresh", [P, PACK], F32)
        gain = tile("gain", [P, PACK], F32)
        with nc.allow_non_contiguous_dma(reason="one float32 value a row"):
            for held, source in ((slope, sl), (thresh, th), (gain, gs)):
                nc.gpsimd.dma_start(held[:], source.rearrange("(u p) o -> p (u o)", p=P))
        slope_thresh = tile("slope_thresh", [P, PACK], F32)
        bias = tile("bias", [P, PACK], F32)
        nc.gpsimd.tensor_tensor(slope_thresh[:], slope[:], thresh[:], ALU.mult)
        nc.gpsimd.tensor_scalar(bias[:], slope_thresh[:], -1.0, 0.0, ALU.mult, ALU.add)
        ident = tile("ident", [P, P], F32)
        make_identity(nc, ident[:])

        planes_first = tile("planes_first", [P, 3 * LIST_HALF + 3 * S], U8)
        planes_second = tile("planes_second", [P, 3 * LIST_HALF], U8)
        planes_cand = tile("planes_cand", [P, C], U8)
        for planes in (planes_first, planes_second, planes_cand):
            nc.vector.memset(planes[:].bitcast(I32), 0)

        def seat_rows(queues, planes, picked):
            for s in range(4):
                queues[s % len(queues)].dma_start(planes.bitcast(I32)[s:P:32, :], picked.bitcast(I32)[8 * s:P:32, :])

        d_names = ("k1", "k2", "k3")
        x_names = ("offs", "two", "hz")

        def d_cols(g):
            return slice(g * LIST_HALF, (g + 1) * LIST_HALF)

        def x_cols(g):
            return slice(3 * LIST_HALF + g * S, 3 * LIST_HALF + (g + 1) * S)

        def pick_d_bytes(half, picked):
            for g, name in enumerate(d_names):
                offsets = entries(name, half * LIST_HALF, (half + 1) * LIST_HALF)
                nc.vector.tensor_copy(picked[:, d_cols(g)], d_bytes[:].indirect(offsets))

        def pick_d_words(half, afters):
            picked = []
            for name, after in zip(d_names, afters):
                words = tile(f"d_words_{name}_{half}", [P, LIST_HALF], U32, after=after)
                offsets = entries(name, half * LIST_HALF, (half + 1) * LIST_HALF)
                nc.vector.tensor_copy(words[:], d_table[:].indirect(offsets))
                picked.append(words)
            return picked

        def first_products(half, d_picked, d_planes):
            sums = [psum.tile([P, S], F32, name=f"h_sum{u}", tag=f"bank{u}") for u in (2 * half, 2 * half + 1)]
            for v in range(2):
                for g in range(3):
                    nc.tensor.matmul_mx(
                        out=sums[v][:],
                        lhsT=d_picked[g][:, v * P:(v + 1) * P].bitcast(FP8X4),
                        lhsT_scale=d_planes[:, g * LIST_HALF + v * P:g * LIST_HALF + (v + 1) * P],
                        rhs=x_picked[g][:].bitcast(FP8X4),
                        rhs_scale=planes_first[:, x_cols(g)],
                        start=(g == 0), stop=(g == 2))
            return sums

        bytes_first = tile("bytes_first", [P, 3 * LIST_HALF + 3 * S], U8)
        for name in ("hz", "offs", "two"):
            nc.vector.tensor_copy(bytes_first[:, x_cols(x_names.index(name))], x_bytes[:].indirect(lists[name][:]))
        pick_d_bytes(0, bytes_first)
        seat_rows((nc.scalar, nc.sync), planes_first[:], bytes_first[:])
        load_lists(("n1", n1), ("n2", n2), ("n3", n3), ("n4", n4), ("n5", n5), ("cand", cand))
        x_picked = []
        for name in x_names:
            words = tile("x_words_" + name, [P, S], U32)
            nc.vector.tensor_copy(words[:], x_table[:].indirect(lists[name][:]))
            x_picked.append(words)
        sums_first = first_products(0, pick_d_words(0, (None, None, None)), planes_first)

        bytes_second = tile("bytes_second", [P, 3 * LIST_HALF], U8, after="bytes_first")
        pick_d_bytes(1, bytes_second)
        seat_rows((nc.sync,), planes_second[:], bytes_second[:])

        def fetch_pair(u, h_sum):
            h = tile(f"h{u}", [P, S], F32)
            if u == 0:
                nc.scalar.activation(h[:], h_sum[:], ACT.Copy, scale=SIXTEENTH)
            else:
                nc.vector.tensor_scalar(h[:], h_sum[:], SIXTEENTH, None, ALU.mult)
            pair = tile(f"pair{u}", [P, 2, W], F32)
            nc.scalar.activation(pair[:, 0, :], h[:].indirect(lists["n1"][:]), ACT.Copy)
            nc.scalar.activation(pair[:, 1, :], h[:].indirect(lists["n2"][:]), ACT.Copy)
            return pair

        def rank(u, pairs):
            high = [tile(f"high{u + v}", [P, W], F32) for v in range(2)]
            low = [tile(f"low{u}", [P, W], F32, after=f"h{u + 1}"), tile(f"low{u + 1}", [P, W], F32)]
            for v in range(2):
                nc.vector.tensor_tensor(high[v][:], pairs[v][:, 0, :], pairs[v][:, 1, :], ALU.max)
            for v in range(2):
                nc.vector.tensor_tensor(low[v][:], pairs[v][:, 0, :], pairs[v][:, 1, :], ALU.min)
            return high, low

        def put_back(u, high, low):
            for v in range(2):
                nc.scalar.activation(ub[u + v][:].indirect(lists["n3"][:]), high[v][:], ACT.Copy)
            for v in range(2):
                nc.scalar.activation(ub[u + v][:].indirect(lists["n4"][:]), low[v][:], ACT.Copy)

        def fetch_sigmoid(u, sg, lo, hi):
            nc.scalar.activation(sg[:, lo:hi], ub[u][:].indirect(entries("n5", lo, hi)), ACT.Sigmoid,
                                 bias=bias[:, u:u + 1], scale=slope[:, u:u + 1])

        def gate(u, a, sg, z_half):
            cols = slice(a * P, (a + 1) * P)
            nc.vector.scalar_tensor_tensor(
                z_half[:, :, u, :], ub[u][:, cols].rearrange("p (b j) -> p b j", j=RUN), gain[:, u:u + 1],
                sg[:, cols].rearrange("p (b j) -> p b j", j=RUN), ALU.mult, ALU.mult)

        ranked_first = rank(0, [fetch_pair(u, sums_first[u]) for u in range(2)])

        sums_second = first_products(1, pick_d_words(1, ("h0", "pair0", "pair1")), planes_second)
        put_back(0, *ranked_first)
        ranked_second = rank(2, [fetch_pair(2 + v, sums_second[v]) for v in range(2)])

        bytes_cand = tile("bytes_cand", [P, PACK, P], U8, after="pair2")
        nc.vector.tensor_copy(bytes_cand[:].rearrange("p t m -> p m t"), x_bytes[:].indirect(lists["cand"][:]))
        seat_rows((nc.sync,), planes_cand[:], bytes_cand[:].rearrange("p t m -> p (t m)"))
        load_lists(("n6", n6), ("n7", n7), ("n8", n8), ("n9", n9), ("n10", n10))

        z_halves = [tile("z_half0", [P, 2, PACK, RUN], BF16, after="pair1"),
                    tile("z_half1", [P, 2, PACK, RUN], BF16, after="planes_second")]
        for u, after in ((0, None), (1, "h2")):
            sg = tile(f"sg{u}", [P, S], F32, after=after)
            fetch_sigmoid(u, sg, 0, S)
            for a in range(2):
                gate(u, a, sg, z_halves[a])

        words_cand = tile("words_cand", [P, PACK, P], U32, after="pair3")
        for half in range(2):
            nc.vector.tensor_copy(words_cand[:].rearrange("p t m -> p m t")[:, half * P // 2:(half + 1) * P // 2, :],
                                  x_table[:].indirect(entries("cand", half * C // 2, (half + 1) * C // 2)))

        put_back(2, *ranked_second)
        late_sg = {u: tile(f"sg{u}", [P, S], F32) for u in (2, 3)}
        for a in range(2):
            for u in (2, 3):
                fetch_sigmoid(u, late_sg[u], a * P, (a + 1) * P)
                gate(u, a, late_sg[u], z_halves[a])

        z_codes = tile("z_codes", [P, S], U32)
        z_scales = tile("z_scales", [P, S], U8)
        s_sums = [psum.tile([P, S], F32, name=f"s_sum{t}", tag=f"bank{t}") for t in range(PACK)]
        for a in range(2):
            cols = slice(a * P, (a + 1) * P)
            dealt = tile(f"dealt{a}", [P, 2, P], F32)
            for b in range(2):
                turned = psum.tile([P, P], F32, name=f"turned{a}_{b}", tag=f"turned{a}_{b}")
                z_words = z_halves[a][:].rearrange("m b u j -> m (b u j)").bitcast(F32)[:, b * P:(b + 1) * P]
                nc.tensor.transpose(turned[:].rearrange("w (t q) -> w t q", t=PACK), z_words,
                                    ident[:].rearrange("m (q t) -> m t q", t=PACK))
                nc.vector.transpose(dealt[:, b, :], turned[:])
            z_woven = tile(f"z_woven{a}", [P, PACK * P], BF16)
            nc.vector.tensor_copy(
                z_woven[:].rearrange("p (b j t) -> p b j t", b=2, t=PACK),
                dealt[:].rearrange("p b w -> p (b w)").bitcast(BF16).rearrange("p (b t j) -> p b j t", b=2, t=PACK))
            nc.vector.quantize_mx(out=z_codes[:, cols].bitcast(FP8X4), scales=z_scales[:, cols], in_=z_woven[:])
            for t in range(PACK):
                nc.tensor.matmul_mx(
                    out=s_sums[t][:, cols],
                    lhsT=words_cand[:, t, :].bitcast(FP8X4), lhsT_scale=planes_cand[:, t * P:(t + 1) * P],
                    rhs=z_codes[:, cols].bitcast(FP8X4), rhs_scale=z_scales[:, cols], start=True, stop=True)
            if a == 0:
                nc.vector.tensor_scalar(scores[0][:, cols], s_sums[0][:, cols], SIXTEENTH, None, ALU.mult)
            else:
                nc.scalar.activation(scores[0][:, cols], s_sums[0][:, cols], ACT.Copy, scale=SIXTEENTH)
        for t in range(1, PACK):
            nc.vector.tensor_scalar(scores[t][:, :S], s_sums[t][:], SIXTEENTH, None, ALU.mult)

        result = tile("result", [P, PACK, S], F32)
        out_rows = out_0.rearrange("(p t) j -> p t j", t=PACK)

        def place(t):
            pair = tile(f"s_pair{t}", [P, 2, W], F32)
            nc.scalar.activation(pair[:, 0, :], scores[t][:].indirect(lists["n6"][:]), ACT.Copy)
            nc.scalar.activation(pair[:, 1, :], scores[t][:].indirect(lists["n7"][:]), ACT.Copy)
            larger = tile(f"larger{t}", [P, W], F32)
            nc.vector.tensor_tensor(larger[:], pair[:, 0, :], pair[:, 1, :], ALU.max)
            ub2 = tile(f"ub2_{t}", [P, S], F32)
            nc.scalar.activation(ub2[:].indirect(lists["n8"][:]), pair[:, 1, :], ACT.Copy)
            nc.scalar.activation(ub2[:].indirect(lists["n9"][:]), larger[:], ACT.Copy)
            return ub2

        def subtract(t, ub2, after=None):
            other = tile(f"other{t}", [P, S], F32, after=after)
            width = S if t < 2 else S // 2
            for lo in range(0, S, width):
                cols = slice(lo, lo + width)
                nc.scalar.activation(other[:, cols], scores[t][:].indirect(entries("n10", lo, lo + width)), ACT.Copy)
                nc.vector.tensor_tensor(result[:, t, cols], ub2[:, cols], other[:, cols], ALU.subtract)
                nc.sync.dma_start(out_rows[:, t, cols], result[:, t, cols])

        placed = [place(0)]
        for t in range(1, PACK):
            placed.append(place(t))
            subtract(t - 1, placed[t - 1])
        last = PACK - 1
        y_woven = [tile(f"y_woven{a}", [P, P, PACK], BF16) for a in range(2)]
        for a in range(2):
            nc.vector.tensor_copy(y_woven[a][:, :, :last],
                                  result[:, :last, a * P:(a + 1) * P].rearrange("p t j -> p j t"))
        subtract(last, placed[last], after=f"s_pair{last}")

        y_codes = tile("y_codes", [P, S], U32)
        y_scales = tile("y_scales", [P, S], U8)
        codes_out = out_1[0].rearrange("p n t -> p (n t)").bitcast(I32)
        for a in range(2):
            cols = slice(a * P, (a + 1) * P)
            nc.vector.tensor_copy(y_woven[a][:, :, last], result[:, last, cols])
            nc.vector.quantize_mx(out=y_codes[:, cols].bitcast(FP8X4), scales=y_scales[:, cols],
                                  in_=y_woven[a][:].rearrange("p j t -> p (j t)"))
            nc.sync.dma_start(codes_out[:, cols], y_codes[:, cols].bitcast(I32))
        for q in range(4):
            queue = nc.sync if q % 2 else nc.scalar
            queue.dma_start(out_2[0].bitcast(I32)[4 * q:4 * q + 4, :], y_scales[:].bitcast(I32)[32 * q:32 * q + 4, :])
